import numpy as np
import ml_dtypes


def mxq(x, axis, fmt="e4m3"):
    dtype, down = {"e4m3": (ml_dtypes.float8_e4m3fn, 7), "e5m2": (ml_dtypes.float8_e5m2, 14)}[fmt]
    v = np.moveaxis(np.asarray(x, np.float32).astype(ml_dtypes.bfloat16).astype(np.float64), axis, -1)
    blocks = v.reshape(v.shape[:-1] + (-1, 32))
    amax = np.abs(blocks).max(-1, keepdims=True)
    byte = np.maximum(np.where(amax > 0, np.frexp(amax)[1] - 1 + 127, 0) - down, 1)
    scale = np.exp2(byte - 127.0)
    codes = (blocks / scale).astype(np.float32).astype(dtype).astype(np.float64)
    return np.moveaxis((codes * scale).reshape(v.shape), -1, axis)


WIDE = False


def mx_kscale(k):
    if not WIDE:
        return np.ones(k)
    levels = np.array([10, -10, 5, -5, 0])
    if k % 512:
        return np.exp2(np.random.permutation(np.resize(levels, k // 32))).repeat(32)
    a = np.empty((k // 512, 16))
    for p in range(k // 512):
        a[p, :8] = np.random.permutation(np.resize(levels, 8))
        for g in range(8):
            far = levels[np.abs(levels - a[p, g]) >= 10]
            a[p, g + 8] = far[np.random.randint(len(far))]
    return np.exp2(a.ravel()).repeat(32)


def f64(x):
    return np.asarray(x).astype(np.float64)


def striped(idx):
    return np.tile(np.asarray(idx).reshape(-1, 16).T, (8, 1)).astype(np.uint16)


def unstriped(offs):
    return offs[:16].T.reshape(-1).astype(np.int64)


def striped8(idx):
    return np.asarray(idx).reshape(8, -1, 16).transpose(0, 2, 1).reshape(128, -1).astype(np.uint16)


def unstriped8(offs):
    return offs.reshape(8, 16, -1).transpose(0, 2, 1).reshape(8, -1).astype(np.int64)


def pick8(x, idx, run):
    r = np.arange(len(x))
    return x[r[:, None], idx[r % (8 * run) // run]]


E2M1 = np.array([0.0, 0.5, 1.0, 1.5, 2.0, 3.0, 4.0, 6.0, -0.0, -0.5, -1.0, -1.5, -2.0, -3.0, -4.0, -6.0])


def pack_weight(w, fmt):
    k, n = w.shape
    w = f64(np.asarray(w, np.float32).astype(ml_dtypes.bfloat16)).reshape(k // 32, 32, n)
    amax = np.abs(w).max(1)
    if fmt == "e4m3":
        byte = np.frexp(amax)[1] - 1 + 127 - 7
    else:
        mant, ex = np.frexp(amax / 6.0)
        byte = np.where(mant > 0.5, ex, ex - 1) + 127
    byte = np.clip(np.where(amax > 0, byte, 1), 1, 254)
    scaled = (w * np.exp2(127.0 - byte)[:, None, :]).reshape(k, n).astype(np.float32)
    by_word = np.ascontiguousarray(scaled.reshape(k // 512, 128, 4, n).transpose(0, 1, 3, 2))
    if fmt == "e4m3":
        words = by_word.astype(ml_dtypes.float8_e4m3fn).view(np.uint8)
    else:
        c = by_word.astype(ml_dtypes.float4_e2m1fn).view(np.uint8) & 0xF
        words = (c[..., 0::2] | (c[..., 1::2] << 4)).reshape(k // 512, 128, 2 * n)
    return np.ascontiguousarray(words), np.ascontiguousarray(byte.astype(np.uint8).reshape(k // 512, 16, n))


def unpack_weight(words, scales, fmt):
    g, _, n = scales.shape
    words = np.ascontiguousarray(words).reshape(g, 128, n, -1)
    if fmt == "e4m3":
        vals = words.view(ml_dtypes.float8_e4m3fn).astype(np.float64)
    else:
        nib = np.empty((g, 128, n, 4), np.uint8)
        nib[..., 0::2] = words & 0xF
        nib[..., 1::2] = words >> 4
        vals = E2M1[nib]
    vals = vals * np.repeat(np.exp2(scales.astype(np.float64) - 127.0), 8, axis=1)[..., None]
    return vals.transpose(0, 1, 3, 2).reshape(g * 512, n)


K, J, R, T, C, N, U, E, G = 512, 384, 512, 1024, 512, 256, 1024, 256, 512


def setup_inputs():
    n = np.random.standard_normal
    idx = np.random.permutation(T)[:J]
    idx2 = np.stack([np.random.permutation(C)[:J] for _ in range(8)])
    idx3 = np.stack([np.random.permutation(C)[:J] for _ in range(8)])
    idx4 = np.stack([np.random.permutation(U)[:C] for _ in range(8)])
    idx5 = np.stack([np.random.permutation(U)[:E] for _ in range(8)])
    idx6 = np.stack([np.random.permutation(G)[:E] for _ in range(8)])
    fk = mx_kscale(K)
    fr = mx_kscale(R)
    xtp = pack_weight(n((K, T)) * fk[:, None], "e4m3")
    wp = pack_weight(n((K, R)) * 1 / np.sqrt(K) / fk[:, None] * fr, "e4m3")
    w2p = pack_weight(n((K, R)) * 1 / np.sqrt(K) / fk[:, None] * fr, "e2m1")
    wbp = pack_weight(n((R, N)) * 1 / np.sqrt(R) / fr[:, None], "e2m1")
    wop = pack_weight(n((R, N)) * 1 / np.sqrt(R) / fr[:, None], "e4m3")
    return {
        "xt_words": xtp[0],
        "xt_scales": xtp[1],
        "w_words": wp[0],
        "w_scales": wp[1],
        "w2_words": w2p[0],
        "w2_scales": w2p[1],
        "wb_words": wbp[0],
        "wb_scales": wbp[1],
        "wo_words": wop[0],
        "wo_scales": wop[1],
        "se": (np.random.uniform(0.5, 1.6, (N, 1))).astype(np.float32),
        "offs": striped(idx),
        "offs2": striped8(idx2),
        "offs3": striped8(idx3),
        "offs4": striped8(idx4),
        "offs5": striped8(idx5),
        "offs6": striped8(idx6),
    }


def reference(xt_words, xt_scales, w_words, w_scales, w2_words, w2_scales, wb_words, wb_scales, wo_words, wo_scales, se, offs, offs2, offs3, offs4, offs5, offs6):
    idx = unstriped(offs)
    idx2 = unstriped8(offs2)
    idx3 = unstriped8(offs3)
    idx4 = unstriped8(offs4)
    idx5 = unstriped8(offs5)
    idx6 = unstriped8(offs6)
    xtu = unpack_weight(xt_words, xt_scales, "e4m3")
    wu = unpack_weight(w_words, w_scales, "e4m3")
    w2u = unpack_weight(w2_words, w2_scales, "e2m1")
    wbu = unpack_weight(wb_words, wb_scales, "e2m1")
    wou = unpack_weight(wo_words, wo_scales, "e4m3")
    xtidxg = xtu[:, idx]
    a = wu.T @ xtidxg
    b = w2u.T @ xtidxg
    pw = np.zeros((R, C))
    pw[np.arange(R)[:, None], idx2[np.arange(R) % 512 // 64]] = a
    pv = np.zeros((R, C))
    pv[np.arange(R)[:, None], idx3[np.arange(R) % 512 // 64]] = b
    pwq = mxq(pw, 0, "e4m3")
    pvq = mxq(pv, 0, "e4m3")
    p = wbu.T @ pwq + wou.T @ pvq
    m0 = np.zeros((N, U))
    m0[np.arange(N)[:, None], idx4[np.arange(N) % 128 // 16]] = p
    m1 = pick8(m0, idx5, 16) * f64(se)
    y = np.zeros((N, G))
    y[np.arange(N)[:, None], idx6[np.arange(N) % 128 // 16]] = m1
    return y

from contextlib import ExitStack

import concourse.mybir as mybir

K, J, R, T, C, N, U, E, G = 512, 384, 512, 1024, 512, 256, 1024, 256, 512
FLOPS = 2 * (2 * K * R * J) + 2 * (2 * R * N * C)

F32 = mybir.dt.float32
BF16 = mybir.dt.bfloat16
I32 = mybir.dt.int32
U32 = mybir.dt.uint32
U16 = mybir.dt.uint16
U8 = mybir.dt.uint8
FP8X4 = mybir.dt.float8_e4m3fn_x4
FP4X4 = mybir.dt.float4_e2m1fn_x4
COPY = mybir.ActivationFunctionType.Copy

P = 128
PACK = 4
QUADS = 4
LIST_ROWS = 16
ALIGN = 64
SLOT_PARTS = ((0, 128), (128, 384))
PAGE_PARTS = ((0, 128), (128, 256), (256, 384), (384, 512))


def entries(list_tile, lo, hi):
    return list_tile[:, lo // LIST_ROWS : hi // LIST_ROWS]


def tile_picked_tokens_plain_twin_twopages_pages_endrelay_kernel(
    tc, xt_words, xt_scales, w_words, w_scales, w2_words, w2_scales, wb_words, wb_scales,
    wo_words, wo_scales, se, offs, offs2, offs3, offs4, offs5, offs6, out,
):
    nc = tc.nc
    with ExitStack() as ctx:
        lists = ctx.enter_context(tc.tile_pool(name="lists", bufs=1))
        sb = ctx.enter_context(tc.tile_pool(name="sb", bufs=1))
        psum = ctx.enter_context(tc.psum_pool(name="psum", bufs=1))

        def sbuf(name, shape, dtype, tag=None):
            return sb.tile(shape, dtype, name=name, tag=tag or name, align_bytes=ALIGN)

        def bank(name, number, width):
            return psum.tile([P, width], F32, name=name, tag="bank%d" % number)

        def load_list(name, source):
            list_tile = lists.tile(list(source.shape), U16, name=name)
            nc.sync.dma_start(list_tile[:], source)
            return list_tile

        def load_words(name, source, dtype, width, tag=None):
            words = sbuf(name, [P, width], dtype, tag)
            nc.sync.dma_start(out=words[:].bitcast(I32), in_=source.bitcast(I32))
            return words

        def cleared_plane(name, width):
            plane = sbuf(name, [P, width], U8)
            nc.vector.memset(plane[:].bitcast(I32), 0)
            return plane

        def stage_scale_rows(name, source, queue):
            width = source.shape[2] // 4
            staged = sbuf(name, [PACK, QUADS, width], I32)
            queue.dma_start(out=staged[:], in_=source[0].bitcast(I32).rearrange("(q i) w -> i q w", i=PACK))
            return staged

        def spread_scale_rows(plane, staged):
            for q in range(QUADS):
                nc.vector.tensor_copy(out=plane[32 * q : 32 * q + PACK, :].bitcast(I32), in_=staged[:, q, :])

        def load_scale_rows(plane, source):
            for q in range(QUADS):
                nc.sync.dma_start(
                    out=plane[32 * q : 32 * q + PACK, :].bitcast(I32),
                    in_=source[0, PACK * q : PACK * (q + 1), :].bitcast(I32),
                )

        x_staged = sbuf("x_staged", [P, 2, T // 4], I32)
        for half in range(2):
            nc.scalar.dma_start(
                out=x_staged[64 * half : 64 * half + PACK, :, :],
                in_=xt_scales[0, 8 * half : 8 * half + 8, :].bitcast(I32).rearrange("(q i) w -> i q w", i=PACK),
            )
        w2_staged = stage_scale_rows("w2_staged", w2_scales, nc.sync)
        token_list = load_list("token_list", offs)
        w2_raw = load_words("w2_raw", w2_words[0], U8, 2 * R)
        x_words = load_words("x_words", xt_words[0].rearrange("p n t -> p (n t)"), U32, T)
        pv_list = load_list("pv_list", offs3)
        w_raw = load_words("w_raw", w_words[0].rearrange("p n t -> p (n t)"), I32, R)
        w_staged = stage_scale_rows("w_staged", w_scales, nc.sync)
        pw_list = load_list("pw_list", offs2)

        x_plane = cleared_plane("x_plane", T)
        w2_plane = cleared_plane("w2_plane", R)
        pv = [sbuf("pv%d" % t, [P, C], F32) for t in range(PACK)]
        for t in range(PACK):
            nc.vector.memset(pv[t][:], 0.0)
        wo_plane = cleared_plane("wo_plane", N)
        wb_plane = cleared_plane("wb_plane", N)

        wo_codes = load_words("wo_codes", wo_words[0].rearrange("p n t -> p (n t)"), I32, N)
        load_scale_rows(wo_plane, wo_scales)
        wb_codes = load_words("wb_codes", wb_words[0], U8, 2 * N)
        load_scale_rows(wb_plane, wb_scales)
        relay_put_list = load_list("relay_put_list", offs4)
        relay_get_list = load_list("relay_get_list", offs5)
        last_list = load_list("last_list", offs6)
        gains = []
        for h in range(N // P):
            gain = sbuf("gain%d" % h, [P, 1], F32)
            nc.sync.dma_start(out=gain[:], in_=se[P * h : P * (h + 1), :])
            gains.append(gain)

        for q in range(QUADS):
            nc.vector.tensor_copy(
                out=x_plane[32 * q : 32 * q + PACK, :].bitcast(I32),
                in_=x_staged[64 * (q // 2) : 64 * (q // 2) + PACK, q % 2, :],
            )
        picked_words, picked_scales = [], []

        def gather_scales(part):
            lo, hi = SLOT_PARTS[part]
            picked = sbuf("picked_scales%d" % part, [P, hi - lo], U8, ("picked_scales0", "b0_0")[part])
            nc.vector.tensor_copy(out=picked[:], in_=x_plane[:].indirect(entries(token_list, lo, hi)))
            picked_scales.append(picked)

        def gather_words(part):
            lo, hi = SLOT_PARTS[part]
            picked = sbuf("picked_words%d" % part, [P, hi - lo], U32)
            nc.vector.tensor_copy(out=picked[:], in_=x_words[:].indirect(entries(token_list, lo, hi)))
            picked_words.append(picked)

        w2_dealt = sbuf("w2_dealt", [P, PACK, 2 * P], U8, "dealt_words")
        w2_dealt_scales = sbuf("w2_dealt_scales", [P, PACK, P], U8, "dealt_scales")
        w2_by_tile = w2_raw[:].bitcast(U16).rearrange("p (m t) -> p t m", t=PACK)
        w2_plane_by_tile = w2_plane[:].rearrange("p (m t) -> p t m", t=PACK)

        gather_scales(0)
        spread_scale_rows(w2_plane, w2_staged)
        nc.vector.tensor_copy(out=w2_dealt_scales[:, 0, :], in_=w2_plane_by_tile[:, 0, :])
        gather_words(0)
        nc.vector.tensor_copy(out=w2_dealt_scales[:, 1:, :], in_=w2_plane_by_tile[:, 1:, :])
        nc.scalar.copy(out=w2_dealt[:].bitcast(U16), in_=w2_by_tile)

        def product_b(t, part):
            lo, hi = SLOT_PARTS[part]
            acc = bank("b_acc%d_%d" % (t, part), PACK * part + t, hi - lo)
            nc.tensor.matmul_mx(
                out=acc[:], lhsT=w2_dealt[:, t, :].bitcast(FP4X4), lhsT_scale=w2_dealt_scales[:, t, :],
                rhs=picked_words[part][:].bitcast(FP8X4), rhs_scale=picked_scales[part][:],
                start=True, stop=True,
            )
            values = sbuf("b%d_%d" % (t, part), [P, hi - lo], F32)
            if t == 0 and part == 0:
                nc.scalar.activation(out=values[:], in_=acc[:], func=COPY)
            else:
                nc.vector.tensor_copy(out=values[:], in_=acc[:])
            nc.scalar.activation(out=pv[t][:].indirect(entries(pv_list, lo, hi)), in_=values[:], func=COPY)

        for t in range(PACK):
            product_b(t, 0)
        gather_words(1)
        gather_scales(1)
        for t in range(PACK):
            product_b(t, 1)

        w_plane = sbuf("w_plane", [P, R], U8, "x_plane")
        nc.vector.memset(w_plane[:].bitcast(I32), 0)
        spread_scale_rows(w_plane, w_staged)
        w_dealt = sbuf("w_dealt", [P, PACK, P], I32, "dealt_words")
        w_dealt_scales = sbuf("w_dealt_scales", [P, PACK, P], U8, "dealt_scales")
        nc.vector.tensor_copy(out=w_dealt_scales[:], in_=w_plane[:].rearrange("p (m t) -> p t m", t=PACK))
        nc.vector.tensor_copy(out=w_dealt[:], in_=w_raw[:].rearrange("p (m t) -> p t m", t=PACK))

        a_values = []
        for t in range(PACK):
            acc = bank("a_acc%d" % t, t, J)
            for part, (lo, hi) in enumerate(SLOT_PARTS):
                nc.tensor.matmul_mx(
                    out=acc[:, lo:hi], lhsT=w_dealt[:, t, :].bitcast(FP8X4), lhsT_scale=w_dealt_scales[:, t, :],
                    rhs=picked_words[part][:].bitcast(FP8X4), rhs_scale=picked_scales[part][:],
                    start=True, stop=True,
                )
            values = sbuf("a%d" % t, [P, J], F32)
            nc.vector.tensor_copy(out=values[:], in_=acc[:])
            a_values.append(values)

        freed = ["w_raw", "x_plane", "dealt_words", "dealt_scales"]
        pw = [sbuf("pw%d" % t, [P, C], F32, freed[t]) for t in range(PACK)]
        relay = [sbuf("relay%d" % h, [P, U], F32, "picked_words%d" % h) for h in range(N // P)]
        last = [sbuf("last%d" % h, [P, G], F32, ("picked_scales0", "b0_0")[h]) for h in range(N // P)]
        for window in pw + relay + last:
            nc.vector.memset(window[:], 0.0)
        for t in range(PACK):
            nc.scalar.activation(out=pw[t][:].indirect(pw_list[:]), in_=a_values[t][:], func=COPY)

        pv_woven = sbuf("pv_woven", [P, C, PACK], BF16)
        for t in range(PACK):
            nc.vector.tensor_copy(out=pv_woven[:, :, t], in_=pv[t][:])
        pv_codes = sbuf("pv_codes", [P, C], U32)
        pv_scales = sbuf("pv_scales", [P, C], U8)
        nc.vector.quantize_mx(
            out=pv_codes[:].bitcast(FP8X4), scales=pv_scales[:], in_=pv_woven[:].rearrange("p c t -> p (c t)")
        )
        sums = {}
        for part, (lo, hi) in enumerate(PAGE_PARTS):
            for h in range(N // P):
                acc = bank("p_acc%d_%d" % (part, h), 2 * part + h, hi - lo)
                nc.tensor.matmul_mx(
                    out=acc[:], lhsT=wo_codes[:, P * h : P * (h + 1)].bitcast(FP8X4),
                    lhsT_scale=wo_plane[:, P * h : P * (h + 1)],
                    rhs=pv_codes[:, lo:hi].bitcast(FP8X4), rhs_scale=pv_scales[:, lo:hi],
                    start=True, stop=False,
                )
                sums[(part, h)] = acc

        woven = sbuf("pw_woven0", [P, P, PACK], BF16, "pw_woven")
        rounded = sbuf("pw_rounded", [P, PACK, C - P], BF16)
        for t in range(PACK):
            nc.vector.tensor_copy(out=woven[:, :, t], in_=pw[t][:, :P])
            nc.vector.tensor_copy(out=rounded[:, t, :], in_=pw[t][:, P:])
        for part, (lo, hi) in enumerate(PAGE_PARTS):
            if part > 0:
                woven = sbuf("pw_woven%d" % part, [P, P, PACK], BF16, "pw_woven")
                nc.vector.tensor_copy(out=woven[:], in_=rounded[:, :, lo - P : hi - P].rearrange("p t c -> p c t"))
            pw_codes = sbuf("pw_codes%d" % part, [P, hi - lo], U32)
            pw_scales = sbuf("pw_scales%d" % part, [P, hi - lo], U8)
            nc.vector.quantize_mx(
                out=pw_codes[:].bitcast(FP8X4), scales=pw_scales[:], in_=woven[:].rearrange("p c t -> p (c t)")
            )
            for h in range(N // P):
                acc = sums[(part, h)]
                nc.tensor.matmul_mx(
                    out=acc[:], lhsT=wb_codes[:, 2 * P * h : 2 * P * (h + 1)].bitcast(FP4X4),
                    lhsT_scale=wb_plane[:, P * h : P * (h + 1)],
                    rhs=pw_codes[:].bitcast(FP8X4), rhs_scale=pw_scales[:],
                    start=False, stop=True,
                )
                values = sbuf("p%d_%d" % (part, h), [P, hi - lo], F32)
                if part == 0 and h == 0:
                    nc.scalar.activation(out=values[:], in_=acc[:], func=COPY)
                else:
                    nc.vector.tensor_copy(out=values[:], in_=acc[:])
                nc.scalar.activation(
                    out=relay[h][:].indirect(entries(relay_put_list, lo, hi)), in_=values[:], func=COPY
                )

        relayed = []
        for h in range(N // P):
            fetched = sbuf("relayed%d" % h, [P, E], F32)
            nc.scalar.activation(out=fetched[:], in_=relay[h][:].indirect(relay_get_list[:]), func=COPY, scale=gains[h][:])
            relayed.append(fetched)
        for h in range(N // P):
            nc.scalar.activation(out=last[h][:].indirect(last_list[:]), in_=relayed[h][:], func=COPY)
            nc.sync.dma_start(out=out[P * h : P * (h + 1), :], in_=last[h][:])
